import numpy as np
import ml_dtypes


def mxq(x, axis, fmt="e4m3"):
    dtype, down = {"e4m3": (ml_dtypes.float8_e4m3fn, 7), "e5m2": (ml_dtypes.float8_e5m2, 14)}[fmt]
    v = np.moveaxis(np.asarray(x, np.float32).astype(ml_dtypes.bfloat16).astype(np.float64), axis, -1)
    blocks = v.reshape(v.shape[:-1] + (-1, 32))
    amax = np.abs(blocks).max(-1, keepdims=True)
    byte = np.maximum(np.where(amax > 0, np.frexp(amax)[1] - 1 + 127, 0) - down, 1)
    scale = np.exp2(byte - 127.0)
    codes = (blocks / scale).astype(np.float32).astype(dtype).astype(np.float64)
    return np.moveaxis((codes * scale).reshape(v.shape), -1, axis)


WIDE = False


def mx_kscale(k):
    if not WIDE:
        return np.ones(k)
    levels = np.array([10, -10, 5, -5, 0])
    if k % 512:
        return np.exp2(np.random.permutation(np.resize(levels, k // 32))).repeat(32)
    a = np.empty((k // 512, 16))
    for p in range(k // 512):
        a[p, :8] = np.random.permutation(np.resize(levels, 8))
        for g in range(8):
            far = levels[np.abs(levels - a[p, g]) >= 10]
            a[p, g + 8] = far[np.random.randint(len(far))]
    return np.exp2(a.ravel()).repeat(32)


def f64(x):
    return np.asarray(x).astype(np.float64)


def striped(idx):
    return np.tile(idx.reshape(-1, 16).T, (8, 1)).astype(np.uint16)


def unstriped(offs):
    return offs[:16].T.reshape(-1).astype(np.int64)


E2M1 = np.array([0.0, 0.5, 1.0, 1.5, 2.0, 3.0, 4.0, 6.0, -0.0, -0.5, -1.0, -1.5, -2.0, -3.0, -4.0, -6.0])


def pack_weight(w, fmt):
    k, n = w.shape
    w = f64(np.asarray(w, np.float32).astype(ml_dtypes.bfloat16)).reshape(k // 32, 32, n)
    amax = np.abs(w).max(1)
    if fmt == "e4m3":
        byte = np.frexp(amax)[1] - 1 + 127 - 7
    else:
        mant, ex = np.frexp(amax / 6.0)
        byte = np.where(mant > 0.5, ex, ex - 1) + 127
    byte = np.clip(np.where(amax > 0, byte, 1), 1, 254)
    scaled = (w * np.exp2(127.0 - byte)[:, None, :]).reshape(k, n).astype(np.float32)
    by_word = np.ascontiguousarray(scaled.reshape(k // 512, 128, 4, n).transpose(0, 1, 3, 2))
    if fmt == "e4m3":
        words = by_word.astype(ml_dtypes.float8_e4m3fn).view(np.uint8)
    else:
        c = by_word.astype(ml_dtypes.float4_e2m1fn).view(np.uint8) & 0xF
        words = (c[..., 0::2] | (c[..., 1::2] << 4)).reshape(k // 512, 128, 2 * n)
    return np.ascontiguousarray(words), np.ascontiguousarray(byte.astype(np.uint8).reshape(k // 512, 16, n))


def unpack_weight(words, scales, fmt):
    g, _, n = scales.shape
    words = np.ascontiguousarray(words).reshape(g, 128, n, -1)
    if fmt == "e4m3":
        vals = words.view(ml_dtypes.float8_e4m3fn).astype(np.float64)
    else:
        nib = np.empty((g, 128, n, 4), np.uint8)
        nib[..., 0::2] = words & 0xF
        nib[..., 1::2] = words >> 4
        vals = E2M1[nib]
    vals = vals * np.repeat(np.exp2(scales.astype(np.float64) - 127.0), 8, axis=1)[..., None]
    return vals.transpose(0, 1, 3, 2).reshape(g * 512, n)


def gelu(v):
    return 0.5 * v * (1.0 + np.tanh(np.sqrt(2.0 / np.pi) * (v + 0.044715 * v**3)))


def striped8(idx):
    return np.concatenate([v.reshape(-1, 16).T for v in idx]).astype(np.uint16)


def unstriped8(offs):
    return np.stack([offs[16 * g:16 * g + 16].T.reshape(-1) for g in range(8)]).astype(np.int64)


def heads(h, wgt, idx8):
    r = np.arange(h.shape[0])
    return wgt[r // 4 % 128] * h[r[:, None], idx8[r % 512 // 64]]


def put_heads(h, wgs, idx8, t2):
    r = np.arange(h.shape[0])
    page = np.zeros((h.shape[0], t2))
    page[r[:, None], idx8[r % 512 // 64]] = wgs[r // 4 % 128] * h
    return page


K, T, S, H, P, T2 = 512, 4096, 1024, 1024, 512, 1024


def setup_inputs():
    n = np.random.standard_normal
    s = mx_kscale(K)[:, None]
    u = mx_kscale(H)[:, None]
    d = {}
    d["tab_words"], d["tab_scales"] = pack_weight(n((K, T)) * s, "e4m3")
    d["offs"] = striped(np.random.permutation(T)[:S])
    d["w1"] = (n((K, H)) / K ** 0.5 / s).astype(np.float32)
    d["w2_words"], d["w2_scales"] = pack_weight(n((K, H)) / K ** 0.5 / s, "e2m1")
    d["w3"] = (n((K, H)) / K ** 0.5 / s).astype(np.float32)
    d["offs2"] = striped8(np.stack([np.random.permutation(S)[:P] for _ in range(8)]))
    d["wgt"] = np.repeat(np.random.uniform(0.5, 2.0, (8, P)), 16, axis=0).astype(np.float32)
    d["gain"] = (np.exp(0.4 * n(H)) * u[:, 0]).astype(np.float32)
    d["w4_words"], d["w4_scales"] = pack_weight(n((H, H)) / H ** 0.5 / u, "e4m3")
    d["offs3"] = striped8(np.stack([np.random.permutation(T2)[:P] for _ in range(8)]))
    d["wgo"] = np.repeat(np.random.uniform(0.5, 2.0, (8, P)), 16, axis=0).astype(np.float32)
    return d


def reference(tab_words, tab_scales, offs, w1, w2_words, w2_scales, w3, offs2, wgt, gain, w4_words, w4_scales, offs3, wgo):
    v = unpack_weight(tab_words, tab_scales, "e4m3")[:, unstriped(offs)]
    lost = mxq(f64(w1), 0, "e4m3").T @ v
    idle = unpack_weight(w2_words, w2_scales, "e2m1").T @ v
    done = mxq(f64(w3), 0, "e4m3").T @ v
    h = np.maximum(lost, idle) - done
    x = heads(h, f64(wgt), unstriped8(offs2))
    z = mxq(x * f64(gain)[:, None], 0, "e4m3")
    room = unpack_weight(w4_words, w4_scales, "e4m3").T @ z
    y = np.minimum(room, x)
    return put_heads(y, f64(wgo), unstriped8(offs3), T2)

@@ -1,0 +1,310 @@
+from contextlib import ExitStack
+
+import concourse.mybir as mybir
+
+K, T, S, H, M, T2 = 512, 4096, 1024, 1024, 512, 1024
+FLOPS = 3 * 2 * K * H * S + 2 * H * H * M
+
+F32 = mybir.dt.float32
+BF16 = mybir.dt.bfloat16
+I32 = mybir.dt.int32
+U32 = mybir.dt.uint32
+U16 = mybir.dt.uint16
+U8 = mybir.dt.uint8
+FP8X4 = mybir.dt.float8_e4m3fn_x4
+FP4X4 = mybir.dt.float4_e2m1fn_x4
+ALU = mybir.AluOpType
+COPY = mybir.ActivationFunctionType.Copy
+
+P = 128
+PACK = 4
+RUN = P * PACK
+RUNS = H // RUN
+BANK = 512
+HALVES = S // BANK
+HM = M // 2
+
+
+def tile_list_room_hint_urgency_kernel(
+    tc, tab_words, tab_scales, offs, w1, w2_words, w2_scales, w3, offs2, wgt, gain, w4_words, w4_scales, offs3, wgo, out
+):
+    nc = tc.nc
+    with ExitStack() as ctx:
+        lists = ctx.enter_context(tc.tile_pool(name="lists", bufs=1))
+        keep = ctx.enter_context(tc.tile_pool(name="keep", bufs=1))
+        ring = ctx.enter_context(tc.tile_pool(name="ring", bufs=2))
+        psum = ctx.enter_context(tc.psum_pool(name="psum", bufs=1))
+
+        def held(shape, dtype, name, tag=None):
+            return keep.tile(shape, dtype, name=name, tag=tag or name, align_bytes=64)
+
+        offs_sb = lists.tile([P, S // 16], U16, name="offs_sb")
+        offs2_sb = lists.tile([P, M // 16], U16, name="offs2_sb")
+        offs3_sb = lists.tile([P, M // 16], U16, name="offs3_sb")
+
+        tab_w = held([P, T], I32, "tab_w")
+        tab_s = held([P, T], U8, "tab_s")
+        w2_w = held([P, 2 * H], U8, "w2_w")
+        w_s = held([P, H], U8, "w_s")
+        raw = {}
+        pages = {(b, t): held([P, T2], F32, "page%d%d" % (b, t)) for b in range(RUNS) for t in range(PACK)}
+
+        nc.vector.memset(w_s[:].bitcast(I32), 0)
+        nc.vector.memset(tab_s[:].bitcast(I32), 0)
+
+        def load_weight(n, w, b, parts):
+            width = RUN // parts
+            for u in range(parts):
+                raw[n, b, u] = held([P, PACK, width], F32, "raw%d%d%d" % (n, b, u), "raw%d%d" % (n, u))
+                c0 = b * RUN + u * width
+                nc.sync.dma_start(out=raw[n, b, u][:], in_=w[:, c0 : c0 + width].rearrange("(p j) c -> p j c", j=PACK))
+
+        nc.sync.dma_start(offs_sb[:], offs)
+        nc.sync.dma_start(offs2_sb[:], offs2)
+        nc.sync.dma_start(offs3_sb[:], offs3)
+        load_weight(1, w1, 0, 1)
+        for q in range(4):
+            nc.sync.dma_start(
+                out=w_s[32 * q : 32 * q + 4, :].bitcast(I32), in_=w2_scales[0, 4 * q : 4 * q + 4, :].bitcast(I32)
+            )
+        nc.sync.dma_start(out=w2_w[:].bitcast(I32), in_=w2_words[0].bitcast(I32))
+        for q in range(4):
+            nc.scalar.dma_start(
+                out=tab_s[32 * q : 32 * q + 4, :].bitcast(I32), in_=tab_scales[0, 4 * q : 4 * q + 4, :].bitcast(I32)
+            )
+        nc.sync.dma_start(out=tab_w[:], in_=tab_words[0].rearrange("p t i -> p (t i)").bitcast(I32))
+        load_weight(3, w3, 0, 1)
+
+        for page in pages.values():
+            nc.vector.memset(page[:], 0.0)
+
+        grouped, codes, scales = {}, {}, {}
+
+        def cast_views(n, b, u, parts):
+            if u == 0:
+                grouped[n, b] = ring.tile([P, PACK * RUN], BF16, name="grouped", align_bytes=64)
+            q = P // parts
+            dst = grouped[n, b][:].rearrange("p (t q j) -> p q t j", t=PACK, j=PACK)[:, u * q : (u + 1) * q]
+            src = raw[n, b, u][:].rearrange("p j (q t) -> p q t j", t=PACK)
+            return dst, src
+
+        def cast_scalar(n, b, parts=1):
+            for u in range(parts):
+                dst, src = cast_views(n, b, u, parts)
+                nc.scalar.activation(out=dst, in_=src, func=COPY)
+
+        def cast_gpsimd(n, b):
+            dst, src = cast_views(n, b, 0, 1)
+            nc.gpsimd.tensor_scalar(out=dst, in0=src, scalar1=1.0, scalar2=0.0, op0=ALU.mult, op1=ALU.add)
+
+        def quantize_weight(n, b):
+            codes[n, b] = held([P, RUN], U32, "codes%d%d" % (n, b))
+            scales[n, b] = held([P, RUN], U8, "scales%d%d" % (n, b))
+            nc.vector.quantize_mx(out=codes[n, b][:].bitcast(FP8X4), scales=scales[n, b][:], in_=grouped[n, b][:])
+
+        v_w = {}
+        v_s = held([P, S], U8, "v_s")
+        w2_dw = held([P, 2 * H], U8, "w2_dw")
+        w2_ds = held([P, H], U8, "w2_ds")
+        w4_dw = held([P, RUNS * H], I32, "w4_dw")
+        w4_ds = held([P, H], U8, "w4_ds")
+
+        def gather_words(g):
+            cols = slice(g * BANK // 16, (g + 1) * BANK // 16)
+            v_w[g] = held([P, BANK], U32, "v_w%d" % g, "tab_s" if g == 0 else None)
+            nc.vector.tensor_copy(v_w[g][:], tab_w[:].bitcast(U32).indirect(offs_sb[:, cols]))
+
+        def deal(dst, src):
+            nc.vector.tensor_copy(
+                out=dst.rearrange("p (b t q) -> p b t q", t=PACK, q=P),
+                in_=src.rearrange("p (b q t) -> p b t q", t=PACK, q=P),
+            )
+
+        def deal_w2(b):
+            deal(
+                w2_dw[:, 2 * b * RUN : 2 * (b + 1) * RUN].bitcast(U16),
+                w2_w[:, 2 * b * RUN : 2 * (b + 1) * RUN].bitcast(U16),
+            )
+            deal(w2_ds[:, b * RUN : (b + 1) * RUN], w_s[:, b * RUN : (b + 1) * RUN])
+
+        def first_product(lhsT, lhsT_scale, g, tag, bufs):
+            bank = psum.tile([P, BANK], F32, name=tag, bufs=bufs)
+            nc.tensor.matmul_mx(
+                out=bank[:],
+                lhsT=lhsT,
+                lhsT_scale=lhsT_scale,
+                rhs=v_w[g][:].bitcast(FP8X4),
+                rhs_scale=v_s[:, g * BANK : (g + 1) * BANK],
+                start=True,
+                stop=True,
+            )
+            return bank
+
+        h = {(b, t): held([P, S], F32, "h%d%d" % (b, t)) for b in range(RUNS) for t in range(PACK)}
+
+        def worse(b, t, g):
+            cols = slice(t * P, (t + 1) * P)
+            lost = first_product(codes[1, b][:, cols].bitcast(FP8X4), scales[1, b][:, cols], g, "bank_a", 2)
+            c0 = b * RUN + t * P
+            idle = first_product(
+                w2_dw[:, 2 * c0 : 2 * (c0 + P)].bitcast(FP4X4), w2_ds[:, c0 : c0 + P], g, "bank_b", 3
+            )
+            lost_sb = ring.tile([P, BANK], F32, name="lost_sb", tag="staged", bufs=4, align_bytes=64)
+            nc.scalar.activation(out=lost_sb[:], in_=lost[:], func=COPY)
+            nc.vector.tensor_tensor(h[b, t][:, g * BANK : (g + 1) * BANK], lost_sb[:], idle[:], ALU.max)
+
+        def less_done(b, t, g):
+            cols = slice(t * P, (t + 1) * P)
+            done = first_product(codes[3, b][:, cols].bitcast(FP8X4), scales[3, b][:, cols], g, "bank_c", 3)
+            part = h[b, t][:, g * BANK : (g + 1) * BANK]
+            nc.vector.tensor_tensor(part, part, done[:], ALU.subtract)
+
+        x = {}
+        planes = {}
+
+        def pick(b, t, lo, n, xt):
+            x[b, t, lo] = xt
+            window = h[b, t][:].indirect(offs2_sb[:, lo // 16 : (lo + n) // 16])
+            nc.vector.tensor_tensor(xt[:], window, wgt_sb[:, lo : lo + n], ALU.mult)
+            if (b, lo) not in planes:
+                planes[b, lo] = held([P, PACK, n], BF16, "planes%d%d" % (b, lo))
+            nc.scalar.activation(out=planes[b, lo][:, t, :], in_=xt[:], func=COPY, scale=gain_sb[:, b, t : t + 1])
+
+        z_in, z_w, z_s = {}, {}, {}
+
+        def weave(b, lo, n):
+            z_in[b, lo] = held([P, PACK * n], BF16, "z_in%d%d" % (b, lo))
+            nc.scalar.copy(
+                out=z_in[b, lo][:].rearrange("p (c i t) -> p c t i", i=4, t=PACK),
+                in_=planes[b, lo][:].rearrange("p t (c i) -> p c t i", i=4),
+            )
+
+        def quantize_z(b, lo, n):
+            if b not in z_w:
+                z_w[b] = held([P, M], U32, "z_w%d" % b)
+                z_s[b] = held([P, M], U8, "z_s%d" % b)
+            nc.vector.quantize_mx(
+                out=z_w[b][:, lo : lo + n].bitcast(FP8X4), scales=z_s[b][:, lo : lo + n], in_=z_in[b, lo][:]
+            )
+
+        cast_scalar(1, 0)
+        nc.vector.tensor_copy(v_s[:], tab_s[:].indirect(offs_sb[:]))
+        quantize_weight(1, 0)
+        load_weight(1, w1, 1, 1)
+        deal_w2(0)
+        deal_w2(1)
+        factors = held([P, 2 * M + RUNS * PACK], F32, "factors", "w2_w")
+        wgt_sb = factors[:, 0:M]
+        wgo_sb = factors[:, M : 2 * M]
+        gain_sb = factors[:, 2 * M :].rearrange("p (b i) -> p b i", b=RUNS)
+        nc.sync.dma_start(out=wgt_sb, in_=wgt)
+        nc.sync.dma_start(out=gain_sb, in_=gain.rearrange("(b p i) -> p b i", b=RUNS, i=PACK))
+        gather_words(0)
+        gather_words(1)
+        cast_gpsimd(3, 0)
+        w4_w = held([P, RUNS * H], I32, "w4_w", "tab_w")
+        nc.sync.dma_start(
+            out=w4_w[:].rearrange("p (a c) -> p a c", a=RUNS),
+            in_=w4_words.rearrange("a p c i -> p a (c i)").bitcast(I32),
+        )
+        load_weight(3, w3, 1, 1)
+        for q in range(4):
+            nc.sync.dma_start(
+                out=w_s[32 * q + 4 : 32 * q + 12, :].bitcast(I32), in_=w4_scales[:, 4 * q : 4 * q + 4, :].bitcast(I32)
+            )
+        nc.sync.dma_start(out=wgo_sb, in_=wgo)
+
+        for g in range(HALVES):
+            for t in range(PACK):
+                worse(0, t, g)
+            if g == 0:
+                quantize_weight(3, 0)
+        cast_scalar(1, 1)
+        for t in range(PACK):
+            less_done(0, t, 0)
+            if t > 0:
+                pick(0, t - 1, 0, M, held([P, M], F32, "x0%d" % (t - 1)))
+            less_done(0, t, 1)
+            if t == 1:
+                quantize_weight(1, 1)
+                cast_scalar(3, 1)
+        quantize_weight(3, 1)
+
+        for t in range(PACK):
+            worse(1, t, 0)
+            worse(1, t, 1)
+            if t == 0:
+                pick(0, PACK - 1, 0, M, held([P, M], F32, "x03"))
+                weave(0, 0, M)
+            else:
+                pick(1, t - 1, 0, HM, held([P, HM], F32, "x1%d" % (t - 1)))
+            if t == 1:
+                nc.vector.tensor_copy(
+                    out=w4_dw[:].rearrange("p (a t c i) -> p a c t i", t=PACK, c=P // 4, i=4),
+                    in_=w4_w[:].rearrange("p (a c i t) -> p a c t i", t=PACK, c=P // 4, i=4),
+                )
+                deal(w4_ds[:], w_s[:])
+            if t == 2:
+                quantize_z(0, 0, M)
+            less_done(1, t, 0)
+            less_done(1, t, 1)
+
+        def late_x():
+            return ring.tile([P, HM], F32, name="x_late", tag="staged", bufs=4, align_bytes=64)
+
+        pick(1, 0, HM, HM, late_x())
+        pick(1, PACK - 1, 0, HM, held([P, HM], F32, "x13"))
+        weave(1, 0, HM)
+        for t in range(1, PACK):
+            pick(1, t, HM, HM, late_x())
+        weave(1, HM, HM)
+        quantize_z(1, 0, HM)
+
+        rows = out.rearrange("(b p i) c -> b i p c", b=RUNS, i=PACK)
+        tags = (("bank_a", 2), ("bank_b", 3), ("bank_c", 3))
+        count = []
+
+        def room(b, t, lo, n):
+            tag, bufs = tags[len(count) % 3]
+            count.append(0)
+            bank = psum.tile([P, BANK], F32, name=tag, bufs=bufs)
+            c0 = b * RUN + t * P
+            for a in range(RUNS):
+                nc.tensor.matmul_mx(
+                    out=bank[:, 0:n],
+                    lhsT=w4_dw[:, a * H + c0 : a * H + c0 + P].bitcast(FP8X4),
+                    lhsT_scale=w4_ds[4 * a + 4 : P, c0 : c0 + P],
+                    rhs=z_w[a][:, lo : lo + n].bitcast(FP8X4),
+                    rhs_scale=z_s[a][:, lo : lo + n],
+                    start=(a == 0),
+                    stop=(a == RUNS - 1),
+                )
+            return bank
+
+        def capped(b, t, lo, n):
+            bank = room(b, t, lo, n)
+            y = ring.tile([P, n], F32, name="y", tag="y", bufs=3, align_bytes=64)
+            if b == 0:
+                nc.vector.tensor_tensor(y[:], x[b, t, 0][:], bank[:, 0:n], ALU.min)
+            else:
+                for c in range(0, n, HM):
+                    nc.vector.tensor_tensor(y[:, c : c + HM], x[b, t, lo + c][:], bank[:, c : c + HM], ALU.min)
+            return y
+
+        def place(b, t, lo, n, y):
+            window = pages[b, t][:].indirect(offs3_sb[:, lo // 16 : (lo + n) // 16])
+            nc.vector.tensor_tensor(window, y[:], wgo_sb[:, lo : lo + n], ALU.mult)
+            if lo + n == M:
+                nc.sync.dma_start(out=rows[b, t], in_=pages[b, t][:])
+
+        steps = [(1, 0, 0, HM), (1, 1, 0, HM), (1, 0, HM, HM), (1, 1, HM, HM), (1, 2, 0, M), (1, 3, 0, M)]
+        steps = steps + [(0, t, 0, M) for t in range(PACK)]
+        pending = None
+        for i, step in enumerate(steps):
+            if i == 2:
+                quantize_z(1, HM, HM)
+            y = capped(*step)
+            if pending is not None:
+                place(*pending)
+            pending = step + (y,)
+        place(*pending)

@@ -47,24 +47,21 @@ def tile_list_room_hint_urgency_kernel(
         w2_w = held([P, 2 * H], U8, "w2_w")
         w_s = held([P, H], U8, "w_s")
         raw = {}
-        pages = {(b, t): held([P, T2], F32, "page%d%d" % (b, t)) for b in range(RUNS) for t in range(PACK)}
+        pages = {}
 
-        nc.vector.memset(w_s[:].bitcast(I32), 0)
+        nc.gpsimd.memset(w_s[:].bitcast(I32), 0)
         nc.vector.memset(tab_s[:].bitcast(I32), 0)
 
-        def load_weight(n, w, b, parts):
-            width = RUN // parts
-            for u in range(parts):
-                raw[n, b, u] = held([P, PACK, width], F32, "raw%d%d%d" % (n, b, u), "raw%d%d" % (n, u))
-                c0 = b * RUN + u * width
-                nc.sync.dma_start(out=raw[n, b, u][:], in_=w[:, c0 : c0 + width].rearrange("(p j) c -> p j c", j=PACK))
+        def load_weight(n, w, b, tag):
+            raw[n, b] = held([P, PACK, RUN], F32, "raw%d%d" % (n, b), tag)
+            nc.sync.dma_start(out=raw[n, b][:], in_=w[:, b * RUN : (b + 1) * RUN].rearrange("(p j) c -> p j c", j=PACK))
 
         nc.sync.dma_start(offs_sb[:], offs)
         nc.sync.dma_start(offs2_sb[:], offs2)
         nc.sync.dma_start(offs3_sb[:], offs3)
-        load_weight(1, w1, 0, 1)
+        load_weight(1, w1, 0, "raw_a")
         for q in range(4):
-            nc.sync.dma_start(
+            nc.gpsimd.dma_start(
                 out=w_s[32 * q : 32 * q + 4, :].bitcast(I32), in_=w2_scales[0, 4 * q : 4 * q + 4, :].bitcast(I32)
             )
         nc.sync.dma_start(out=w2_w[:].bitcast(I32), in_=w2_words[0].bitcast(I32))
@@ -73,46 +70,39 @@ def tile_list_room_hint_urgency_kernel(
                 out=tab_s[32 * q : 32 * q + 4, :].bitcast(I32), in_=tab_scales[0, 4 * q : 4 * q + 4, :].bitcast(I32)
             )
         nc.sync.dma_start(out=tab_w[:], in_=tab_words[0].rearrange("p t i -> p (t i)").bitcast(I32))
-        load_weight(3, w3, 0, 1)
-
-        for page in pages.values():
-            nc.vector.memset(page[:], 0.0)
+        load_weight(3, w3, 0, "raw_b")
 
         grouped, codes, scales = {}, {}, {}
 
-        def cast_views(n, b, u, parts):
+        def cast_views(n, b, u, parts, tag):
             if u == 0:
-                grouped[n, b] = ring.tile([P, PACK * RUN], BF16, name="grouped", align_bytes=64)
-            q = P // parts
-            dst = grouped[n, b][:].rearrange("p (t q j) -> p q t j", t=PACK, j=PACK)[:, u * q : (u + 1) * q]
-            src = raw[n, b, u][:].rearrange("p j (q t) -> p q t j", t=PACK)
+                grouped[n, b] = held([P, PACK * RUN], BF16, "grouped%d%d" % (n, b), tag)
+            qs = slice(u * P // parts, (u + 1) * P // parts)
+            dst = grouped[n, b][:].rearrange("p (t q j) -> p q t j", t=PACK, j=PACK)[:, qs]
+            src = raw[n, b][:].rearrange("p j (q t) -> p q t j", t=PACK)[:, qs]
             return dst, src
 
-        def cast_scalar(n, b, parts=1):
-            for u in range(parts):
-                dst, src = cast_views(n, b, u, parts)
-                nc.scalar.activation(out=dst, in_=src, func=COPY)
+        def cast_scalar(n, b, u=0, parts=1):
+            dst, src = cast_views(n, b, u, parts, "grouped_s" if b else None)
+            nc.scalar.activation(out=dst, in_=src, func=COPY)
 
-        def cast_gpsimd(n, b):
-            dst, src = cast_views(n, b, 0, 1)
+        def cast_gpsimd(n, b, u=0, parts=1):
+            dst, src = cast_views(n, b, u, parts, "grouped_g")
             nc.gpsimd.tensor_scalar(out=dst, in0=src, scalar1=1.0, scalar2=0.0, op0=ALU.mult, op1=ALU.add)
 
         def quantize_weight(n, b):
-            codes[n, b] = held([P, RUN], U32, "codes%d%d" % (n, b))
+            codes[n, b] = held([P, RUN], U32, "codes%d%d" % (n, b), "tab_s" if (n, b) == (1, 0) else None)
             scales[n, b] = held([P, RUN], U8, "scales%d%d" % (n, b))
             nc.vector.quantize_mx(out=codes[n, b][:].bitcast(FP8X4), scales=scales[n, b][:], in_=grouped[n, b][:])
 
-        v_w = {}
         v_s = held([P, S], U8, "v_s")
         w2_dw = held([P, 2 * H], U8, "w2_dw")
         w2_ds = held([P, H], U8, "w2_ds")
         w4_dw = held([P, RUNS * H], I32, "w4_dw")
-        w4_ds = held([P, H], U8, "w4_ds")
 
         def gather_words(g):
             cols = slice(g * BANK // 16, (g + 1) * BANK // 16)
-            v_w[g] = held([P, BANK], U32, "v_w%d" % g, "tab_s" if g == 0 else None)
-            nc.vector.tensor_copy(v_w[g][:], tab_w[:].bitcast(U32).indirect(offs_sb[:, cols]))
+            nc.vector.tensor_copy(v_w[:, g * BANK : (g + 1) * BANK], tab_w[:].bitcast(U32).indirect(offs_sb[:, cols]))
 
         def deal(dst, src):
             nc.vector.tensor_copy(
@@ -133,7 +123,7 @@ def tile_list_room_hint_urgency_kernel(
                 out=bank[:],
                 lhsT=lhsT,
                 lhsT_scale=lhsT_scale,
-                rhs=v_w[g][:].bitcast(FP8X4),
+                rhs=v_w[:, g * BANK : (g + 1) * BANK].bitcast(FP8X4),
                 rhs_scale=v_s[:, g * BANK : (g + 1) * BANK],
                 start=True,
                 stop=True,
@@ -142,6 +132,8 @@ def tile_list_room_hint_urgency_kernel(
 
         h = {(b, t): held([P, S], F32, "h%d%d" % (b, t)) for b in range(RUNS) for t in range(PACK)}
 
+        successor = {(0, 3, 0): "codes30", (0, 1, 1): "grouped_s"}
+
         def worse(b, t, g):
             cols = slice(t * P, (t + 1) * P)
             lost = first_product(codes[1, b][:, cols].bitcast(FP8X4), scales[1, b][:, cols], g, "bank_a", 2)
@@ -149,7 +141,10 @@ def tile_list_room_hint_urgency_kernel(
             idle = first_product(
                 w2_dw[:, 2 * c0 : 2 * (c0 + P)].bitcast(FP4X4), w2_ds[:, c0 : c0 + P], g, "bank_b", 3
             )
-            lost_sb = ring.tile([P, BANK], F32, name="lost_sb", tag="staged", bufs=4, align_bytes=64)
+            if (b, t, g) in successor:
+                lost_sb = held([P, BANK], F32, "lost_held%d" % g, successor[b, t, g])
+            else:
+                lost_sb = ring.tile([P, BANK], F32, name="lost_sb", bufs=6, align_bytes=64)
             nc.scalar.activation(out=lost_sb[:], in_=lost[:], func=COPY)
             nc.vector.tensor_tensor(h[b, t][:, g * BANK : (g + 1) * BANK], lost_sb[:], idle[:], ALU.max)
 
@@ -162,10 +157,14 @@ def tile_list_room_hint_urgency_kernel(
         x = {}
         planes = {}
 
-        def pick(b, t, lo, n, xt):
+        def pick(b, t, lo, n, xt, fused=True):
             x[b, t, lo] = xt
             window = h[b, t][:].indirect(offs2_sb[:, lo // 16 : (lo + n) // 16])
-            nc.vector.tensor_tensor(xt[:], window, wgt_sb[:, lo : lo + n], ALU.mult)
+            if fused:
+                nc.vector.tensor_tensor(xt[:], window, wgt_sb[:, lo : lo + n], ALU.mult)
+            else:
+                nc.vector.tensor_copy(xt[:], window)
+                nc.gpsimd.tensor_tensor(xt[:], xt[:], wgt_sb[:, lo : lo + n], ALU.mult)
             if (b, lo) not in planes:
                 planes[b, lo] = held([P, PACK, n], BF16, "planes%d%d" % (b, lo))
             nc.scalar.activation(out=planes[b, lo][:, t, :], in_=xt[:], func=COPY, scale=gain_sb[:, b, t : t + 1])
@@ -190,7 +189,7 @@ def tile_list_room_hint_urgency_kernel(
         cast_scalar(1, 0)
         nc.vector.tensor_copy(v_s[:], tab_s[:].indirect(offs_sb[:]))
         quantize_weight(1, 0)
-        load_weight(1, w1, 1, 1)
+        load_weight(1, w1, 1, "raw_a")
         deal_w2(0)
         deal_w2(1)
         factors = held([P, 2 * M + RUNS * PACK], F32, "factors", "w2_w")
@@ -199,64 +198,75 @@ def tile_list_room_hint_urgency_kernel(
         gain_sb = factors[:, 2 * M :].rearrange("p (b i) -> p b i", b=RUNS)
         nc.sync.dma_start(out=wgt_sb, in_=wgt)
         nc.sync.dma_start(out=gain_sb, in_=gain.rearrange("(b p i) -> p b i", b=RUNS, i=PACK))
+        v_w = held([P, S], U32, "v_w", "grouped10")
         gather_words(0)
         gather_words(1)
         cast_gpsimd(3, 0)
-        w4_w = held([P, RUNS * H], I32, "w4_w", "tab_w")
-        nc.sync.dma_start(
-            out=w4_w[:].rearrange("p (a c) -> p a c", a=RUNS),
-            in_=w4_words.rearrange("a p c i -> p a (c i)").bitcast(I32),
-        )
-        load_weight(3, w3, 1, 1)
+        load_weight(3, w3, 1, "tab_w")
         for q in range(4):
             nc.sync.dma_start(
                 out=w_s[32 * q + 4 : 32 * q + 12, :].bitcast(I32), in_=w4_scales[:, 4 * q : 4 * q + 4, :].bitcast(I32)
             )
         nc.sync.dma_start(out=wgo_sb, in_=wgo)
 
+        def clear_page(b, t, tag):
+            pages[b, t] = held([P, T2], F32, "page%d%d" % (b, t), tag)
+            nc.gpsimd.memset(pages[b, t][:], 0.0)
+
         for g in range(HALVES):
             for t in range(PACK):
                 worse(0, t, g)
             if g == 0:
                 quantize_weight(3, 0)
-        cast_scalar(1, 1)
+                clear_page(0, 0, "grouped_g")
         for t in range(PACK):
             less_done(0, t, 0)
-            if t > 0:
-                pick(0, t - 1, 0, M, held([P, M], F32, "x0%d" % (t - 1)))
             less_done(0, t, 1)
             if t == 1:
                 quantize_weight(1, 1)
                 cast_scalar(3, 1)
-        quantize_weight(3, 1)
+            if t == 3:
+                quantize_weight(3, 1)
+                clear_page(0, 1, "grouped_s")
+            if t > 0:
+                pick(0, t - 1, 0, M, held([P, M], F32, "x0%d" % (t - 1)))
+                clear_page(1, t - 1, "h0%d" % (t - 1))
+            if t == 0:
+                cast_scalar(1, 1)
+        w4_w = held([P, RUNS * H], I32, "w4_w", "raw_a")
+        nc.sync.dma_start(
+            out=w4_w[:].rearrange("p (a c) -> p a c", a=RUNS),
+            in_=w4_words.rearrange("a p c i -> p a (c i)").bitcast(I32),
+        )
 
         for t in range(PACK):
             worse(1, t, 0)
             worse(1, t, 1)
+            less_done(1, t, 0)
+            less_done(1, t, 1)
             if t == 0:
                 pick(0, PACK - 1, 0, M, held([P, M], F32, "x03"))
+                clear_page(1, PACK - 1, "h03")
                 weave(0, 0, M)
             else:
                 pick(1, t - 1, 0, HM, held([P, HM], F32, "x1%d" % (t - 1)))
             if t == 1:
+                w4_ds = held([P, H], U8, "w4_ds", "scales30")
+                deal(w4_ds[:], w_s[:])
                 nc.vector.tensor_copy(
                     out=w4_dw[:].rearrange("p (a t c i) -> p a c t i", t=PACK, c=P // 4, i=4),
                     in_=w4_w[:].rearrange("p (a c i t) -> p a c t i", t=PACK, c=P // 4, i=4),
                 )
-                deal(w4_ds[:], w_s[:])
+                clear_page(0, 2, "raw_a")
             if t == 2:
                 quantize_z(0, 0, M)
-            less_done(1, t, 0)
-            less_done(1, t, 1)
+                clear_page(0, 3, "z_in00")
 
-        def late_x():
-            return ring.tile([P, HM], F32, name="x_late", tag="staged", bufs=4, align_bytes=64)
-
-        pick(1, 0, HM, HM, late_x())
-        pick(1, PACK - 1, 0, HM, held([P, HM], F32, "x13"))
+        freed = ("codes11", "w2_dw", "w2_ds", "codes31")
+        pick(1, PACK - 1, 0, HM, held([P, HM], F32, "x13"), fused=True)
         weave(1, 0, HM)
-        for t in range(1, PACK):
-            pick(1, t, HM, HM, late_x())
+        for t in range(PACK):
+            pick(1, t, HM, HM, held([P, HM], F32, "x_late%d" % t, freed[t]))
         weave(1, HM, HM)
         quantize_z(1, 0, HM)
 

@@ -15,6 +15,8 @@ FP8X4 = mybir.dt.float8_e4m3fn_x4
 FP4X4 = mybir.dt.float4_e2m1fn_x4
 ALU = mybir.AluOpType
 COPY = mybir.ActivationFunctionType.Copy
+RELU = mybir.ActivationFunctionType.Relu
+FUSED = tuple((1, t, g) for t in (1, 2, 3) for g in (0, 1))
 
 P = 128
 PACK = 4
@@ -47,9 +49,10 @@ def tile_list_room_hint_urgency_kernel(
         w2_w = held([P, 2 * H], U8, "w2_w")
         w_s = held([P, H], U8, "w_s")
         raw = {}
-        pages = {}
+        pages = {(b, t): held([P, T2], F32, "page%d%d" % (b, t)) for b in range(RUNS) for t in range(PACK)}
+        gain_sb = held([P, RUNS, PACK], F32, "gain_sb")
 
-        nc.gpsimd.memset(w_s[:].bitcast(I32), 0)
+        nc.vector.memset(w_s[:].bitcast(I32), 0)
         nc.vector.memset(tab_s[:].bitcast(I32), 0)
 
         def load_weight(n, w, b, tag):
@@ -59,36 +62,34 @@ def tile_list_room_hint_urgency_kernel(
         nc.sync.dma_start(offs_sb[:], offs)
         nc.sync.dma_start(offs2_sb[:], offs2)
         nc.sync.dma_start(offs3_sb[:], offs3)
-        load_weight(1, w1, 0, "raw_a")
+        nc.sync.dma_start(out=gain_sb[:], in_=gain.rearrange("(b p i) -> p b i", b=RUNS, i=PACK))
         for q in range(4):
-            nc.gpsimd.dma_start(
+            if q == 3:
+                load_weight(1, w1, 0, "raw_a")
+            nc.sync.dma_start(
                 out=w_s[32 * q : 32 * q + 4, :].bitcast(I32), in_=w2_scales[0, 4 * q : 4 * q + 4, :].bitcast(I32)
             )
-        nc.sync.dma_start(out=w2_w[:].bitcast(I32), in_=w2_words[0].bitcast(I32))
         for q in range(4):
-            nc.scalar.dma_start(
+            nc.sync.dma_start(
                 out=tab_s[32 * q : 32 * q + 4, :].bitcast(I32), in_=tab_scales[0, 4 * q : 4 * q + 4, :].bitcast(I32)
             )
+        nc.sync.dma_start(out=w2_w[:].bitcast(I32), in_=w2_words[0].bitcast(I32))
         nc.sync.dma_start(out=tab_w[:], in_=tab_words[0].rearrange("p t i -> p (t i)").bitcast(I32))
         load_weight(3, w3, 0, "raw_b")
 
+        for page in pages.values():
+            nc.vector.memset(page[:], 0.0)
+
         grouped, codes, scales = {}, {}, {}
 
-        def cast_views(n, b, u, parts, tag):
-            if u == 0:
-                grouped[n, b] = held([P, PACK * RUN], BF16, "grouped%d%d" % (n, b), tag)
-            qs = slice(u * P // parts, (u + 1) * P // parts)
-            dst = grouped[n, b][:].rearrange("p (t q j) -> p q t j", t=PACK, j=PACK)[:, qs]
-            src = raw[n, b][:].rearrange("p j (q t) -> p q t j", t=PACK)[:, qs]
-            return dst, src
-
-        def cast_scalar(n, b, u=0, parts=1):
-            dst, src = cast_views(n, b, u, parts, "grouped_s" if b else None)
-            nc.scalar.activation(out=dst, in_=src, func=COPY)
-
-        def cast_gpsimd(n, b, u=0, parts=1):
-            dst, src = cast_views(n, b, u, parts, "grouped_g")
-            nc.gpsimd.tensor_scalar(out=dst, in0=src, scalar1=1.0, scalar2=0.0, op0=ALU.mult, op1=ALU.add)
+        def cast(n, b, tag):
+            grouped[n, b] = held([P, PACK * RUN], BF16, "grouped%d%d" % (n, b), tag)
+            nc.scalar.activation(
+                out=grouped[n, b][:].rearrange("p (t q j) -> p q t j", t=PACK, j=PACK),
+                in_=raw[n, b][:].rearrange("p j (q t) -> p q t j", t=PACK),
+                func=COPY,
+                scale=-1.0 if n == 1 else 1.0,
+            )
 
         def quantize_weight(n, b):
             codes[n, b] = held([P, RUN], U32, "codes%d%d" % (n, b), "tab_s" if (n, b) == (1, 0) else None)
@@ -117,41 +118,56 @@ def tile_list_room_hint_urgency_kernel(
             )
             deal(w2_ds[:, b * RUN : (b + 1) * RUN], w_s[:, b * RUN : (b + 1) * RUN])
 
-        def first_product(lhsT, lhsT_scale, g, tag, bufs):
+        def stationary(n, b, t):
+            if n == 2:
+                c0 = b * RUN + t * P
+                return w2_dw[:, 2 * c0 : 2 * (c0 + P)].bitcast(FP4X4), w2_ds[:, c0 : c0 + P]
+            cols = slice(t * P, (t + 1) * P)
+            return codes[n, b][:, cols].bitcast(FP8X4), scales[n, b][:, cols]
+
+        def product(weights, b, t, g, tag, bufs):
             bank = psum.tile([P, BANK], F32, name=tag, bufs=bufs)
-            nc.tensor.matmul_mx(
-                out=bank[:],
-                lhsT=lhsT,
-                lhsT_scale=lhsT_scale,
-                rhs=v_w[:, g * BANK : (g + 1) * BANK].bitcast(FP8X4),
-                rhs_scale=v_s[:, g * BANK : (g + 1) * BANK],
-                start=True,
-                stop=True,
-            )
+            for i, n in enumerate(weights):
+                lhsT, lhsT_scale = stationary(n, b, t)
+                nc.tensor.matmul_mx(
+                    out=bank[:],
+                    lhsT=lhsT,
+                    lhsT_scale=lhsT_scale,
+                    rhs=v_w[:, g * BANK : (g + 1) * BANK].bitcast(FP8X4),
+                    rhs_scale=v_s[:, g * BANK : (g + 1) * BANK],
+                    start=(i == 0),
+                    stop=(i == len(weights) - 1),
+                )
             return bank
 
         h = {(b, t): held([P, S], F32, "h%d%d" % (b, t)) for b in range(RUNS) for t in range(PACK)}
 
         successor = {(0, 3, 0): "codes30", (0, 1, 1): "grouped_s"}
 
-        def worse(b, t, g):
-            cols = slice(t * P, (t + 1) * P)
-            lost = first_product(codes[1, b][:, cols].bitcast(FP8X4), scales[1, b][:, cols], g, "bank_a", 2)
-            c0 = b * RUN + t * P
-            idle = first_product(
-                w2_dw[:, 2 * c0 : 2 * (c0 + P)].bitcast(FP4X4), w2_ds[:, c0 : c0 + P], g, "bank_b", 3
-            )
+        def staged(b, t, g):
             if (b, t, g) in successor:
-                lost_sb = held([P, BANK], F32, "lost_held%d" % g, successor[b, t, g])
-            else:
-                lost_sb = ring.tile([P, BANK], F32, name="lost_sb", bufs=6, align_bytes=64)
-            nc.scalar.activation(out=lost_sb[:], in_=lost[:], func=COPY)
-            nc.vector.tensor_tensor(h[b, t][:, g * BANK : (g + 1) * BANK], lost_sb[:], idle[:], ALU.max)
+                return held([P, BANK], F32, "staged%d%d%d" % (b, t, g), successor[b, t, g])
+            return ring.tile([P, BANK], F32, name="staged", bufs=6, align_bytes=64)
+
+        def worse(b, t, g):
+            if (b, t, g) in FUSED:
+                return
+            minus_lost = product((1,), b, t, g, "bank_a", 2)
+            idle = product((2,), b, t, g, "bank_b", 3)
+            lost = staged(b, t, g)
+            nc.scalar.activation(out=lost[:], in_=minus_lost[:], func=COPY, scale=-1.0)
+            nc.vector.tensor_tensor(h[b, t][:, g * BANK : (g + 1) * BANK], lost[:], idle[:], ALU.max)
 
         def less_done(b, t, g):
-            cols = slice(t * P, (t + 1) * P)
-            done = first_product(codes[3, b][:, cols].bitcast(FP8X4), scales[3, b][:, cols], g, "bank_c", 3)
             part = h[b, t][:, g * BANK : (g + 1) * BANK]
+            if (b, t, g) in FUSED:
+                idle_over = product((1, 2), b, t, g, "bank_b", 3)
+                done_over = product((1, 3), b, t, g, "bank_c", 3)
+                excess = staged(b, t, g)
+                nc.scalar.activation(out=excess[:], in_=idle_over[:], func=RELU)
+                nc.vector.tensor_tensor(part, excess[:], done_over[:], ALU.subtract)
+                return
+            done = product((3,), b, t, g, "bank_c", 3)
             nc.vector.tensor_tensor(part, part, done[:], ALU.subtract)
 
         x = {}
@@ -186,22 +202,28 @@ def tile_list_room_hint_urgency_kernel(
                 out=z_w[b][:, lo : lo + n].bitcast(FP8X4), scales=z_s[b][:, lo : lo + n], in_=z_in[b, lo][:]
             )
 
-        cast_scalar(1, 0)
+        cast(1, 0, None)
         nc.vector.tensor_copy(v_s[:], tab_s[:].indirect(offs_sb[:]))
         quantize_weight(1, 0)
         load_weight(1, w1, 1, "raw_a")
         deal_w2(0)
         deal_w2(1)
-        factors = held([P, 2 * M + RUNS * PACK], F32, "factors", "w2_w")
+        factors = held([P, 2 * M], F32, "factors", "w2_w")
         wgt_sb = factors[:, 0:M]
         wgo_sb = factors[:, M : 2 * M]
-        gain_sb = factors[:, 2 * M :].rearrange("p (b i) -> p b i", b=RUNS)
         nc.sync.dma_start(out=wgt_sb, in_=wgt)
-        nc.sync.dma_start(out=gain_sb, in_=gain.rearrange("(b p i) -> p b i", b=RUNS, i=PACK))
         v_w = held([P, S], U32, "v_w", "grouped10")
         gather_words(0)
         gather_words(1)
-        cast_gpsimd(3, 0)
+        grouped[3, 0] = held([P, PACK * RUN], BF16, "grouped30")
+        nc.gpsimd.tensor_scalar(
+            out=grouped[3, 0][:].rearrange("p (t q j) -> p q t j", t=PACK, j=PACK),
+            in0=raw[3, 0][:].rearrange("p j (q t) -> p q t j", t=PACK),
+            scalar1=1.0,
+            scalar2=0.0,
+            op0=ALU.mult,
+            op1=ALU.add,
+        )
         load_weight(3, w3, 1, "tab_w")
         for q in range(4):
             nc.sync.dma_start(
@@ -209,30 +231,23 @@ def tile_list_room_hint_urgency_kernel(
             )
         nc.sync.dma_start(out=wgo_sb, in_=wgo)
 
-        def clear_page(b, t, tag):
-            pages[b, t] = held([P, T2], F32, "page%d%d" % (b, t), tag)
-            nc.gpsimd.memset(pages[b, t][:], 0.0)
-
         for g in range(HALVES):
             for t in range(PACK):
                 worse(0, t, g)
             if g == 0:
                 quantize_weight(3, 0)
-                clear_page(0, 0, "grouped_g")
         for t in range(PACK):
             less_done(0, t, 0)
             less_done(0, t, 1)
             if t == 1:
                 quantize_weight(1, 1)
-                cast_scalar(3, 1)
+                cast(3, 1, "grouped_s")
             if t == 3:
                 quantize_weight(3, 1)
-                clear_page(0, 1, "grouped_s")
             if t > 0:
                 pick(0, t - 1, 0, M, held([P, M], F32, "x0%d" % (t - 1)))
-                clear_page(1, t - 1, "h0%d" % (t - 1))
             if t == 0:
-                cast_scalar(1, 1)
+                cast(1, 1, "grouped_s")
         w4_w = held([P, RUNS * H], I32, "w4_w", "raw_a")
         nc.sync.dma_start(
             out=w4_w[:].rearrange("p (a c) -> p a c", a=RUNS),
@@ -246,7 +261,6 @@ def tile_list_room_hint_urgency_kernel(
             less_done(1, t, 1)
             if t == 0:
                 pick(0, PACK - 1, 0, M, held([P, M], F32, "x03"))
-                clear_page(1, PACK - 1, "h03")
                 weave(0, 0, M)
             else:
                 pick(1, t - 1, 0, HM, held([P, HM], F32, "x1%d" % (t - 1)))
@@ -257,10 +271,8 @@ def tile_list_room_hint_urgency_kernel(
                     out=w4_dw[:].rearrange("p (a t c i) -> p a c t i", t=PACK, c=P // 4, i=4),
                     in_=w4_w[:].rearrange("p (a c i t) -> p a c t i", t=PACK, c=P // 4, i=4),
                 )
-                clear_page(0, 2, "raw_a")
             if t == 2:
                 quantize_z(0, 0, M)
-                clear_page(0, 3, "z_in00")
 
         freed = ("codes11", "w2_dw", "w2_ds", "codes31")
         pick(1, PACK - 1, 0, HM, held([P, HM], F32, "x13"), fused=True)

@@ -16,15 +16,22 @@ FP4X4 = mybir.dt.float4_e2m1fn_x4
 ALU = mybir.AluOpType
 COPY = mybir.ActivationFunctionType.Copy
 RELU = mybir.ActivationFunctionType.Relu
-FUSED = tuple((1, t, g) for t in (1, 2, 3) for g in (0, 1))
 
 P = 128
 PACK = 4
+LAST = PACK - 1
 RUN = P * PACK
 RUNS = H // RUN
+QUADS = 4
+PER_COLUMN = 16
 BANK = 512
+BANKS = 8
 HALVES = S // BANK
 HM = M // 2
+STAGED_DEPTH = 8
+Y_DEPTH = 3
+
+FOUR_PASS = tuple((RUNS - 1, t, g) for t in range(1, PACK) for g in range(HALVES))
 
 
 def tile_list_room_hint_urgency_kernel(
@@ -34,76 +41,71 @@ def tile_list_room_hint_urgency_kernel(
     with ExitStack() as ctx:
         lists = ctx.enter_context(tc.tile_pool(name="lists", bufs=1))
         keep = ctx.enter_context(tc.tile_pool(name="keep", bufs=1))
-        ring = ctx.enter_context(tc.tile_pool(name="ring", bufs=2))
-        psum = ctx.enter_context(tc.psum_pool(name="psum", bufs=1))
+        ring = ctx.enter_context(tc.tile_pool(name="ring", bufs=1))
+        psum = ctx.enter_context(tc.psum_pool(name="psum", bufs=BANKS))
 
-        def held(shape, dtype, name, tag=None):
-            return keep.tile(shape, dtype, name=name, tag=tag or name, align_bytes=64)
+        def held(shape, dtype, name, after=None):
+            return keep.tile(shape, dtype, name=name, tag=after or name, align_bytes=64)
 
-        offs_sb = lists.tile([P, S // 16], U16, name="offs_sb")
-        offs2_sb = lists.tile([P, M // 16], U16, name="offs2_sb")
-        offs3_sb = lists.tile([P, M // 16], U16, name="offs3_sb")
+        offs_sb = lists.tile([P, S // PER_COLUMN], U16, name="offs_sb")
+        offs2_sb = lists.tile([P, M // PER_COLUMN], U16, name="offs2_sb")
+        offs3_sb = lists.tile([P, M // PER_COLUMN], U16, name="offs3_sb")
 
         tab_w = held([P, T], I32, "tab_w")
         tab_s = held([P, T], U8, "tab_s")
         w2_w = held([P, 2 * H], U8, "w2_w")
         w_s = held([P, H], U8, "w_s")
-        raw = {}
         pages = {(b, t): held([P, T2], F32, "page%d%d" % (b, t)) for b in range(RUNS) for t in range(PACK)}
         gain_sb = held([P, RUNS, PACK], F32, "gain_sb")
 
         nc.vector.memset(w_s[:].bitcast(I32), 0)
         nc.vector.memset(tab_s[:].bitcast(I32), 0)
 
-        def load_weight(n, w, b, tag):
-            raw[n, b] = held([P, PACK, RUN], F32, "raw%d%d" % (n, b), tag)
+        raw = {}
+
+        def load_weight(n, w, b, after):
+            raw[n, b] = held([P, PACK, RUN], F32, "raw%d%d" % (n, b), after)
             nc.sync.dma_start(out=raw[n, b][:], in_=w[:, b * RUN : (b + 1) * RUN].rearrange("(p j) c -> p j c", j=PACK))
+
+        def load_scale_rows(dst, src, quad):
+            nc.sync.dma_start(
+                out=dst[32 * quad : 32 * quad + 4, :].bitcast(I32), in_=src[0, 4 * quad : 4 * quad + 4, :].bitcast(I32)
+            )
 
         nc.sync.dma_start(offs_sb[:], offs)
         nc.sync.dma_start(offs2_sb[:], offs2)
         nc.sync.dma_start(offs3_sb[:], offs3)
-        nc.sync.dma_start(out=gain_sb[:], in_=gain.rearrange("(b p i) -> p b i", b=RUNS, i=PACK))
-        for q in range(4):
-            if q == 3:
-                load_weight(1, w1, 0, "raw_a")
-            nc.sync.dma_start(
-                out=w_s[32 * q : 32 * q + 4, :].bitcast(I32), in_=w2_scales[0, 4 * q : 4 * q + 4, :].bitcast(I32)
-            )
-        for q in range(4):
-            nc.sync.dma_start(
-                out=tab_s[32 * q : 32 * q + 4, :].bitcast(I32), in_=tab_scales[0, 4 * q : 4 * q + 4, :].bitcast(I32)
-            )
+        nc.sync.dma_start(out=gain_sb[:], in_=gain.rearrange("(b p t) -> p b t", b=RUNS, t=PACK))
+        for quad in range(QUADS - 1):
+            load_scale_rows(w_s, w2_scales, quad)
+        load_weight(1, w1, 0, "raw_a")
+        load_scale_rows(w_s, w2_scales, QUADS - 1)
+        for quad in range(QUADS):
+            load_scale_rows(tab_s, tab_scales, quad)
         nc.sync.dma_start(out=w2_w[:].bitcast(I32), in_=w2_words[0].bitcast(I32))
-        nc.sync.dma_start(out=tab_w[:], in_=tab_words[0].rearrange("p t i -> p (t i)").bitcast(I32))
-        load_weight(3, w3, 0, "raw_b")
+        nc.sync.dma_start(out=tab_w[:], in_=tab_words[0].rearrange("p c j -> p (c j)").bitcast(I32))
+        load_weight(3, w3, 0, None)
 
         for page in pages.values():
             nc.vector.memset(page[:], 0.0)
 
         grouped, codes, scales = {}, {}, {}
 
-        def cast(n, b, tag):
-            grouped[n, b] = held([P, PACK * RUN], BF16, "grouped%d%d" % (n, b), tag)
-            nc.scalar.activation(
-                out=grouped[n, b][:].rearrange("p (t q j) -> p q t j", t=PACK, j=PACK),
-                in_=raw[n, b][:].rearrange("p j (q t) -> p q t j", t=PACK),
-                func=COPY,
-                scale=-1.0 if n == 1 else 1.0,
+        def cast_views(n, b):
+            grouped[n, b] = held([P, PACK * RUN], BF16, "grouped%d%d" % (n, b))
+            return (
+                grouped[n, b][:].rearrange("p (t q j) -> p q t j", t=PACK, j=PACK),
+                raw[n, b][:].rearrange("p j (q t) -> p q t j", t=PACK),
             )
 
-        def quantize_weight(n, b):
-            codes[n, b] = held([P, RUN], U32, "codes%d%d" % (n, b), "tab_s" if (n, b) == (1, 0) else None)
+        def cast(n, b):
+            dst, src = cast_views(n, b)
+            nc.scalar.activation(out=dst, in_=src, func=COPY, scale=-1.0 if n == 1 else 1.0)
+
+        def quantize_weight(n, b, after=None):
+            codes[n, b] = held([P, RUN], U32, "codes%d%d" % (n, b), after)
             scales[n, b] = held([P, RUN], U8, "scales%d%d" % (n, b))
             nc.vector.quantize_mx(out=codes[n, b][:].bitcast(FP8X4), scales=scales[n, b][:], in_=grouped[n, b][:])
-
-        v_s = held([P, S], U8, "v_s")
-        w2_dw = held([P, 2 * H], U8, "w2_dw")
-        w2_ds = held([P, H], U8, "w2_ds")
-        w4_dw = held([P, RUNS * H], I32, "w4_dw")
-
-        def gather_words(g):
-            cols = slice(g * BANK // 16, (g + 1) * BANK // 16)
-            nc.vector.tensor_copy(v_w[:, g * BANK : (g + 1) * BANK], tab_w[:].bitcast(U32).indirect(offs_sb[:, cols]))
 
         def deal(dst, src):
             nc.vector.tensor_copy(
@@ -111,12 +113,35 @@ def tile_list_room_hint_urgency_kernel(
                 in_=src.rearrange("p (b q t) -> p b t q", t=PACK, q=P),
             )
 
-        def deal_w2(b):
-            deal(
-                w2_dw[:, 2 * b * RUN : 2 * (b + 1) * RUN].bitcast(U16),
-                w2_w[:, 2 * b * RUN : 2 * (b + 1) * RUN].bitcast(U16),
-            )
+        v_s = held([P, S], U8, "v_s")
+        w2_dw = held([P, 2 * H], U8, "w2_dw")
+        w2_ds = held([P, H], U8, "w2_ds")
+
+        cast(1, 0)
+        nc.vector.tensor_copy(v_s[:], tab_s[:].indirect(offs_sb[:]))
+        quantize_weight(1, 0, after="tab_s")
+        load_weight(1, w1, 1, "raw_a")
+        for b in range(RUNS):
+            words = slice(2 * b * RUN, 2 * (b + 1) * RUN)
+            deal(w2_dw[:, words].bitcast(U16), w2_w[:, words].bitcast(U16))
             deal(w2_ds[:, b * RUN : (b + 1) * RUN], w_s[:, b * RUN : (b + 1) * RUN])
+        factors = held([P, 2 * M], F32, "factors", after="w2_w")
+        wgt_sb = factors[:, 0:M]
+        wgo_sb = factors[:, M : 2 * M]
+        nc.sync.dma_start(out=wgt_sb, in_=wgt)
+        v_w = held([P, S], U32, "v_w", after="grouped10")
+        for g in range(HALVES):
+            entries = offs_sb[:, g * BANK // PER_COLUMN : (g + 1) * BANK // PER_COLUMN]
+            nc.vector.tensor_copy(v_w[:, g * BANK : (g + 1) * BANK], tab_w[:].bitcast(U32).indirect(entries))
+        dst, src = cast_views(3, 0)
+        nc.gpsimd.tensor_scalar(out=dst, in0=src, scalar1=1.0, scalar2=0.0, op0=ALU.mult, op1=ALU.add)
+        load_weight(3, w3, 1, "tab_w")
+        for quad in range(QUADS):
+            nc.sync.dma_start(
+                out=w_s[32 * quad + 4 : 32 * quad + 4 + 4 * RUNS, :].bitcast(I32),
+                in_=w4_scales[:, 4 * quad : 4 * quad + 4, :].bitcast(I32),
+            )
+        nc.sync.dma_start(out=wgo_sb, in_=wgo)
 
         def stationary(n, b, t):
             if n == 2:
@@ -125,8 +150,8 @@ def tile_list_room_hint_urgency_kernel(
             cols = slice(t * P, (t + 1) * P)
             return codes[n, b][:, cols].bitcast(FP8X4), scales[n, b][:, cols]
 
-        def product(weights, b, t, g, tag, bufs):
-            bank = psum.tile([P, BANK], F32, name=tag, bufs=bufs)
+        def product(weights, b, t, g):
+            bank = psum.tile([P, BANK], F32, name="bank")
             for i, n in enumerate(weights):
                 lhsT, lhsT_scale = stationary(n, b, t)
                 nc.tensor.matmul_mx(
@@ -142,53 +167,52 @@ def tile_list_room_hint_urgency_kernel(
 
         h = {(b, t): held([P, S], F32, "h%d%d" % (b, t)) for b in range(RUNS) for t in range(PACK)}
 
-        successor = {(0, 3, 0): "codes30", (0, 1, 1): "grouped_s"}
+        taken_over_by = {
+            (0, 0, 1): "codes30",
+            (0, 1, 1): "grouped11",
+            (0, LAST, 1): "grouped31",
+            (1, LAST, 0): "w4_ds",
+            (1, LAST, 1): "w4_dw",
+        }
 
         def staged(b, t, g):
-            if (b, t, g) in successor:
-                return held([P, BANK], F32, "staged%d%d%d" % (b, t, g), successor[b, t, g])
-            return ring.tile([P, BANK], F32, name="staged", bufs=6, align_bytes=64)
+            if (b, t, g) in taken_over_by:
+                return held([P, BANK], F32, "staged%d%d%d" % (b, t, g), taken_over_by[b, t, g])
+            return ring.tile([P, BANK], F32, name="staged", bufs=STAGED_DEPTH, align_bytes=64)
 
-        def worse(b, t, g):
-            if (b, t, g) in FUSED:
-                return
-            minus_lost = product((1,), b, t, g, "bank_a", 2)
-            idle = product((2,), b, t, g, "bank_b", 3)
+        def larger(b, t, g):
+            minus_lost = product((1,), b, t, g)
+            idle = product((2,), b, t, g)
             lost = staged(b, t, g)
             nc.scalar.activation(out=lost[:], in_=minus_lost[:], func=COPY, scale=-1.0)
             nc.vector.tensor_tensor(h[b, t][:, g * BANK : (g + 1) * BANK], lost[:], idle[:], ALU.max)
 
         def less_done(b, t, g):
             part = h[b, t][:, g * BANK : (g + 1) * BANK]
-            if (b, t, g) in FUSED:
-                idle_over = product((1, 2), b, t, g, "bank_b", 3)
-                done_over = product((1, 3), b, t, g, "bank_c", 3)
-                excess = staged(b, t, g)
-                nc.scalar.activation(out=excess[:], in_=idle_over[:], func=RELU)
-                nc.vector.tensor_tensor(part, excess[:], done_over[:], ALU.subtract)
-                return
-            done = product((3,), b, t, g, "bank_c", 3)
+            done = product((3,), b, t, g)
             nc.vector.tensor_tensor(part, part, done[:], ALU.subtract)
 
-        x = {}
-        planes = {}
+        def four_pass(b, t, g):
+            idle_over_lost = product((1, 2), b, t, g)
+            done_over_lost = product((1, 3), b, t, g)
+            excess = staged(b, t, g)
+            nc.scalar.activation(out=excess[:], in_=idle_over_lost[:], func=RELU)
+            nc.vector.tensor_tensor(h[b, t][:, g * BANK : (g + 1) * BANK], excess[:], done_over_lost[:], ALU.subtract)
 
-        def pick(b, t, lo, n, xt, fused=True):
-            x[b, t, lo] = xt
-            window = h[b, t][:].indirect(offs2_sb[:, lo // 16 : (lo + n) // 16])
-            if fused:
-                nc.vector.tensor_tensor(xt[:], window, wgt_sb[:, lo : lo + n], ALU.mult)
-            else:
-                nc.vector.tensor_copy(xt[:], window)
-                nc.gpsimd.tensor_tensor(xt[:], xt[:], wgt_sb[:, lo : lo + n], ALU.mult)
+        x, planes, z_in, z_w, z_s = {}, {}, {}, {}, {}
+
+        def pick(b, t, lo, n, after=None):
+            x[b, t, lo] = held([P, n], F32, "x%d%d_%d" % (b, t, lo), after)
+            window = h[b, t][:].indirect(offs2_sb[:, lo // PER_COLUMN : (lo + n) // PER_COLUMN])
+            nc.vector.tensor_tensor(x[b, t, lo][:], window, wgt_sb[:, lo : lo + n], ALU.mult)
             if (b, lo) not in planes:
-                planes[b, lo] = held([P, PACK, n], BF16, "planes%d%d" % (b, lo))
-            nc.scalar.activation(out=planes[b, lo][:, t, :], in_=xt[:], func=COPY, scale=gain_sb[:, b, t : t + 1])
-
-        z_in, z_w, z_s = {}, {}, {}
+                planes[b, lo] = held([P, PACK, n], BF16, "planes%d_%d" % (b, lo))
+            nc.scalar.activation(
+                out=planes[b, lo][:, t, :], in_=x[b, t, lo][:], func=COPY, scale=gain_sb[:, b, t : t + 1]
+            )
 
         def weave(b, lo, n):
-            z_in[b, lo] = held([P, PACK * n], BF16, "z_in%d%d" % (b, lo))
+            z_in[b, lo] = held([P, PACK * n], BF16, "z_in%d_%d" % (b, lo))
             nc.scalar.copy(
                 out=z_in[b, lo][:].rearrange("p (c i t) -> p c t i", i=4, t=PACK),
                 in_=planes[b, lo][:].rearrange("p t (c i) -> p c t i", i=4),
@@ -202,130 +226,98 @@ def tile_list_room_hint_urgency_kernel(
                 out=z_w[b][:, lo : lo + n].bitcast(FP8X4), scales=z_s[b][:, lo : lo + n], in_=z_in[b, lo][:]
             )
 
-        cast(1, 0, None)
-        nc.vector.tensor_copy(v_s[:], tab_s[:].indirect(offs_sb[:]))
-        quantize_weight(1, 0)
-        load_weight(1, w1, 1, "raw_a")
-        deal_w2(0)
-        deal_w2(1)
-        factors = held([P, 2 * M], F32, "factors", "w2_w")
-        wgt_sb = factors[:, 0:M]
-        wgo_sb = factors[:, M : 2 * M]
-        nc.sync.dma_start(out=wgt_sb, in_=wgt)
-        v_w = held([P, S], U32, "v_w", "grouped10")
-        gather_words(0)
-        gather_words(1)
-        grouped[3, 0] = held([P, PACK * RUN], BF16, "grouped30")
-        nc.gpsimd.tensor_scalar(
-            out=grouped[3, 0][:].rearrange("p (t q j) -> p q t j", t=PACK, j=PACK),
-            in0=raw[3, 0][:].rearrange("p j (q t) -> p q t j", t=PACK),
-            scalar1=1.0,
-            scalar2=0.0,
-            op0=ALU.mult,
-            op1=ALU.add,
-        )
-        load_weight(3, w3, 1, "tab_w")
-        for q in range(4):
-            nc.sync.dma_start(
-                out=w_s[32 * q + 4 : 32 * q + 12, :].bitcast(I32), in_=w4_scales[:, 4 * q : 4 * q + 4, :].bitcast(I32)
-            )
-        nc.sync.dma_start(out=wgo_sb, in_=wgo)
-
         for g in range(HALVES):
             for t in range(PACK):
-                worse(0, t, g)
-            if g == 0:
-                quantize_weight(3, 0)
+                if (t, g) == (LAST - 1, HALVES - 1):
+                    quantize_weight(3, 0)
+                larger(0, t, g)
+        cast(1, 1)
+        cast(3, 1)
         for t in range(PACK):
             less_done(0, t, 0)
             less_done(0, t, 1)
+            if t > 0:
+                pick(0, t - 1, 0, M)
             if t == 1:
                 quantize_weight(1, 1)
-                cast(3, 1, "grouped_s")
-            if t == 3:
+            if t == 2:
                 quantize_weight(3, 1)
-            if t > 0:
-                pick(0, t - 1, 0, M, held([P, M], F32, "x0%d" % (t - 1)))
-            if t == 0:
-                cast(1, 1, "grouped_s")
-        w4_w = held([P, RUNS * H], I32, "w4_w", "raw_a")
+        w4_w = held([P, RUNS * H], I32, "w4_w", after="raw_a")
         nc.sync.dma_start(
             out=w4_w[:].rearrange("p (a c) -> p a c", a=RUNS),
-            in_=w4_words.rearrange("a p c i -> p a (c i)").bitcast(I32),
+            in_=w4_words.rearrange("a p c j -> p a (c j)").bitcast(I32),
         )
+        pick(0, LAST, 0, M)
+        weave(0, 0, M)
 
         for t in range(PACK):
-            worse(1, t, 0)
-            worse(1, t, 1)
-            less_done(1, t, 0)
-            less_done(1, t, 1)
-            if t == 0:
-                pick(0, PACK - 1, 0, M, held([P, M], F32, "x03"))
-                weave(0, 0, M)
+            if (1, t, 0) in FOUR_PASS:
+                four_pass(1, t, 0)
+                four_pass(1, t, 1)
             else:
-                pick(1, t - 1, 0, HM, held([P, HM], F32, "x1%d" % (t - 1)))
-            if t == 1:
-                w4_ds = held([P, H], U8, "w4_ds", "scales30")
-                deal(w4_ds[:], w_s[:])
-                nc.vector.tensor_copy(
-                    out=w4_dw[:].rearrange("p (a t c i) -> p a c t i", t=PACK, c=P // 4, i=4),
-                    in_=w4_w[:].rearrange("p (a c i t) -> p a c t i", t=PACK, c=P // 4, i=4),
-                )
-            if t == 2:
-                quantize_z(0, 0, M)
-
-        freed = ("codes11", "w2_dw", "w2_ds", "codes31")
-        pick(1, PACK - 1, 0, HM, held([P, HM], F32, "x13"), fused=True)
+                larger(1, t, 0)
+                larger(1, t, 1)
+                less_done(1, t, 0)
+                less_done(1, t, 1)
+            if t > 0:
+                pick(1, t - 1, 0, HM)
+        quantize_z(0, 0, M)
+        pick(1, LAST, 0, HM)
         weave(1, 0, HM)
-        for t in range(PACK):
-            pick(1, t, HM, HM, held([P, HM], F32, "x_late%d" % t, freed[t]))
-        weave(1, HM, HM)
+
+        w4_ds = held([P, H], U8, "w4_ds")
+        deal(w4_ds[:], w_s[:])
+        w4_dw = held([P, RUNS * H], I32, "w4_dw")
+        nc.vector.tensor_copy(
+            out=w4_dw[:].rearrange("p (ab t c i) -> p ab c t i", t=PACK, c=P // 4, i=4),
+            in_=w4_w[:].rearrange("p (ab c i t) -> p ab c t i", t=PACK, c=P // 4, i=4),
+        )
         quantize_z(1, 0, HM)
+        freed_by_those_steps = ("w_s", "raw_a", "planes1_0", "z_in1_0")
+        for t in range(PACK):
+            pick(1, t, HM, HM, after=freed_by_those_steps[t])
+        weave(1, HM, HM)
 
-        rows = out.rearrange("(b p i) c -> b i p c", b=RUNS, i=PACK)
-        tags = (("bank_a", 2), ("bank_b", 3), ("bank_c", 3))
-        count = []
+        rows = out.rearrange("(b p t) c -> b t p c", b=RUNS, t=PACK)
 
-        def room(b, t, lo, n):
-            tag, bufs = tags[len(count) % 3]
-            count.append(0)
-            bank = psum.tile([P, BANK], F32, name=tag, bufs=bufs)
+        def capped(b, t, lo, n, after=None):
+            bank = psum.tile([P, BANK], F32, name="bank")
             c0 = b * RUN + t * P
             for a in range(RUNS):
                 nc.tensor.matmul_mx(
                     out=bank[:, 0:n],
                     lhsT=w4_dw[:, a * H + c0 : a * H + c0 + P].bitcast(FP8X4),
-                    lhsT_scale=w4_ds[4 * a + 4 : P, c0 : c0 + P],
+                    lhsT_scale=w4_ds[4 + 4 * a : P, c0 : c0 + P],
                     rhs=z_w[a][:, lo : lo + n].bitcast(FP8X4),
                     rhs_scale=z_s[a][:, lo : lo + n],
                     start=(a == 0),
                     stop=(a == RUNS - 1),
                 )
-            return bank
-
-        def capped(b, t, lo, n):
-            bank = room(b, t, lo, n)
-            y = ring.tile([P, n], F32, name="y", tag="y", bufs=3, align_bytes=64)
-            if b == 0:
-                nc.vector.tensor_tensor(y[:], x[b, t, 0][:], bank[:, 0:n], ALU.min)
+            if after:
+                y = held([P, n], F32, "y_held", after)
             else:
-                for c in range(0, n, HM):
-                    nc.vector.tensor_tensor(y[:, c : c + HM], x[b, t, lo + c][:], bank[:, c : c + HM], ALU.min)
+                y = ring.tile([P, n], F32, name="y", bufs=Y_DEPTH, align_bytes=64)
+            width = M if b == 0 else HM
+            for c in range(0, n, width):
+                nc.vector.tensor_tensor(y[:, c : c + width], x[b, t, lo + c][:], bank[:, c : c + width], ALU.min)
             return y
 
         def place(b, t, lo, n, y):
-            window = pages[b, t][:].indirect(offs3_sb[:, lo // 16 : (lo + n) // 16])
+            window = pages[b, t][:].indirect(offs3_sb[:, lo // PER_COLUMN : (lo + n) // PER_COLUMN])
             nc.vector.tensor_tensor(window, y[:], wgo_sb[:, lo : lo + n], ALU.mult)
             if lo + n == M:
                 nc.sync.dma_start(out=rows[b, t], in_=pages[b, t][:])
 
-        steps = [(1, 0, 0, HM), (1, 1, 0, HM), (1, 0, HM, HM), (1, 1, HM, HM), (1, 2, 0, M), (1, 3, 0, M)]
+        halved = range(LAST)
+        steps = [(1, t, lo, HM) for lo in (0, HM) for t in halved] + [(1, LAST, 0, M)]
         steps = steps + [(0, t, 0, M) for t in range(PACK)]
         pending = None
-        for i, step in enumerate(steps):
-            if i == 2:
+        for step in steps:
+            if step == (1, halved[-1], 0, HM):
                 quantize_z(1, HM, HM)
-            y = capped(*step)
+                y = capped(*step, after="z_in1_%d" % HM)
+            else:
+                y = capped(*step)
             if pending is not None:
                 place(*pending)
             pending = step + (y,)

from contextlib import ExitStack

import concourse.mybir as mybir

K, T, S, H, M, T2 = 512, 4096, 1024, 1024, 512, 1024
FLOPS = 3 * 2 * K * H * S + 2 * H * H * M

F32 = mybir.dt.float32
BF16 = mybir.dt.bfloat16
I32 = mybir.dt.int32
U32 = mybir.dt.uint32
U16 = mybir.dt.uint16
U8 = mybir.dt.uint8
FP8X4 = mybir.dt.float8_e4m3fn_x4
FP4X4 = mybir.dt.float4_e2m1fn_x4
ALU = mybir.AluOpType
COPY = mybir.ActivationFunctionType.Copy
RELU = mybir.ActivationFunctionType.Relu

P = 128
PACK = 4
LAST = PACK - 1
RUN = P * PACK
RUNS = H // RUN
QUADS = 4
PER_COLUMN = 16
BANK = 512
BANKS = 8
HALVES = S // BANK
HM = M // 2
STAGED_DEPTH = 8
Y_DEPTH = 3

FOUR_PASS = tuple((RUNS - 1, t, g) for t in range(1, PACK) for g in range(HALVES))


def tile_list_room_hint_urgency_kernel(
    tc, tab_words, tab_scales, offs, w1, w2_words, w2_scales, w3, offs2, wgt, gain, w4_words, w4_scales, offs3, wgo, out
):
    nc = tc.nc
    with ExitStack() as ctx:
        lists = ctx.enter_context(tc.tile_pool(name="lists", bufs=1))
        keep = ctx.enter_context(tc.tile_pool(name="keep", bufs=1))
        ring = ctx.enter_context(tc.tile_pool(name="ring", bufs=1))
        psum = ctx.enter_context(tc.psum_pool(name="psum", bufs=BANKS))

        def held(shape, dtype, name, after=None):
            return keep.tile(shape, dtype, name=name, tag=after or name, align_bytes=64)

        offs_sb = lists.tile([P, S // PER_COLUMN], U16, name="offs_sb")
        offs2_sb = lists.tile([P, M // PER_COLUMN], U16, name="offs2_sb")
        offs3_sb = lists.tile([P, M // PER_COLUMN], U16, name="offs3_sb")

        tab_w = held([P, T], I32, "tab_w")
        tab_s = held([P, T], U8, "tab_s")
        w2_w = held([P, 2 * H], U8, "w2_w")
        w_s = held([P, H], U8, "w_s")
        pages = {(b, t): held([P, T2], F32, "page%d%d" % (b, t)) for b in range(RUNS) for t in range(PACK)}
        gain_sb = held([P, RUNS, PACK], F32, "gain_sb")

        nc.vector.memset(w_s[:].bitcast(I32), 0)
        nc.vector.memset(tab_s[:].bitcast(I32), 0)

        raw = {}

        def load_weight(n, w, b, after):
            raw[n, b] = held([P, PACK, RUN], F32, "raw%d%d" % (n, b), after)
            nc.sync.dma_start(out=raw[n, b][:], in_=w[:, b * RUN : (b + 1) * RUN].rearrange("(p j) c -> p j c", j=PACK))

        def load_scale_rows(dst, src, quad):
            nc.sync.dma_start(
                out=dst[32 * quad : 32 * quad + 4, :].bitcast(I32), in_=src[0, 4 * quad : 4 * quad + 4, :].bitcast(I32)
            )

        nc.sync.dma_start(offs_sb[:], offs)
        nc.sync.dma_start(offs2_sb[:], offs2)
        nc.sync.dma_start(offs3_sb[:], offs3)
        nc.sync.dma_start(out=gain_sb[:], in_=gain.rearrange("(b p t) -> p b t", b=RUNS, t=PACK))
        for quad in range(QUADS - 1):
            load_scale_rows(w_s, w2_scales, quad)
        load_weight(1, w1, 0, "raw_a")
        load_scale_rows(w_s, w2_scales, QUADS - 1)
        for quad in range(QUADS):
            load_scale_rows(tab_s, tab_scales, quad)
        nc.sync.dma_start(out=w2_w[:].bitcast(I32), in_=w2_words[0].bitcast(I32))
        nc.sync.dma_start(out=tab_w[:], in_=tab_words[0].rearrange("p c j -> p (c j)").bitcast(I32))
        load_weight(3, w3, 0, None)

        for page in pages.values():
            nc.vector.memset(page[:], 0.0)

        grouped, codes, scales = {}, {}, {}

        def cast_views(n, b):
            grouped[n, b] = held([P, PACK * RUN], BF16, "grouped%d%d" % (n, b))
            return (
                grouped[n, b][:].rearrange("p (t q j) -> p q t j", t=PACK, j=PACK),
                raw[n, b][:].rearrange("p j (q t) -> p q t j", t=PACK),
            )

        def cast(n, b):
            dst, src = cast_views(n, b)
            nc.scalar.activation(out=dst, in_=src, func=COPY, scale=-1.0 if n == 1 else 1.0)

        def quantize_weight(n, b, after=None):
            codes[n, b] = held([P, RUN], U32, "codes%d%d" % (n, b), after)
            scales[n, b] = held([P, RUN], U8, "scales%d%d" % (n, b))
            nc.vector.quantize_mx(out=codes[n, b][:].bitcast(FP8X4), scales=scales[n, b][:], in_=grouped[n, b][:])

        def deal(dst, src):
            nc.vector.tensor_copy(
                out=dst.rearrange("p (b t q) -> p b t q", t=PACK, q=P),
                in_=src.rearrange("p (b q t) -> p b t q", t=PACK, q=P),
            )

        v_s = held([P, S], U8, "v_s")
        w2_dw = held([P, 2 * H], U8, "w2_dw")
        w2_ds = held([P, H], U8, "w2_ds")

        cast(1, 0)
        nc.vector.tensor_copy(v_s[:], tab_s[:].indirect(offs_sb[:]))
        quantize_weight(1, 0, after="tab_s")
        load_weight(1, w1, 1, "raw_a")
        for b in range(RUNS):
            words = slice(2 * b * RUN, 2 * (b + 1) * RUN)
            deal(w2_dw[:, words].bitcast(U16), w2_w[:, words].bitcast(U16))
            deal(w2_ds[:, b * RUN : (b + 1) * RUN], w_s[:, b * RUN : (b + 1) * RUN])
        factors = held([P, 2 * M], F32, "factors", after="w2_w")
        wgt_sb = factors[:, 0:M]
        wgo_sb = factors[:, M : 2 * M]
        nc.sync.dma_start(out=wgt_sb, in_=wgt)
        v_w = held([P, S], U32, "v_w", after="grouped10")
        for g in range(HALVES):
            entries = offs_sb[:, g * BANK // PER_COLUMN : (g + 1) * BANK // PER_COLUMN]
            nc.vector.tensor_copy(v_w[:, g * BANK : (g + 1) * BANK], tab_w[:].bitcast(U32).indirect(entries))
        dst, src = cast_views(3, 0)
        nc.gpsimd.tensor_scalar(out=dst, in0=src, scalar1=1.0, scalar2=0.0, op0=ALU.mult, op1=ALU.add)
        load_weight(3, w3, 1, "tab_w")
        for quad in range(QUADS):
            nc.sync.dma_start(
                out=w_s[32 * quad + 4 : 32 * quad + 4 + 4 * RUNS, :].bitcast(I32),
                in_=w4_scales[:, 4 * quad : 4 * quad + 4, :].bitcast(I32),
            )
        nc.sync.dma_start(out=wgo_sb, in_=wgo)

        def stationary(n, b, t):
            if n == 2:
                c0 = b * RUN + t * P
                return w2_dw[:, 2 * c0 : 2 * (c0 + P)].bitcast(FP4X4), w2_ds[:, c0 : c0 + P]
            cols = slice(t * P, (t + 1) * P)
            return codes[n, b][:, cols].bitcast(FP8X4), scales[n, b][:, cols]

        def product(weights, b, t, g):
            bank = psum.tile([P, BANK], F32, name="bank")
            for i, n in enumerate(weights):
                lhsT, lhsT_scale = stationary(n, b, t)
                nc.tensor.matmul_mx(
                    out=bank[:],
                    lhsT=lhsT,
                    lhsT_scale=lhsT_scale,
                    rhs=v_w[:, g * BANK : (g + 1) * BANK].bitcast(FP8X4),
                    rhs_scale=v_s[:, g * BANK : (g + 1) * BANK],
                    start=(i == 0),
                    stop=(i == len(weights) - 1),
                )
            return bank

        h = {(b, t): held([P, S], F32, "h%d%d" % (b, t)) for b in range(RUNS) for t in range(PACK)}

        taken_over_by = {
            (0, 0, 1): "codes30",
            (0, 1, 1): "grouped11",
            (0, LAST, 1): "grouped31",
            (1, LAST, 0): "w4_ds",
            (1, LAST, 1): "w4_dw",
        }

        def staged(b, t, g):
            if (b, t, g) in taken_over_by:
                return held([P, BANK], F32, "staged%d%d%d" % (b, t, g), taken_over_by[b, t, g])
            return ring.tile([P, BANK], F32, name="staged", bufs=STAGED_DEPTH, align_bytes=64)

        def larger(b, t, g):
            minus_lost = product((1,), b, t, g)
            idle = product((2,), b, t, g)
            lost = staged(b, t, g)
            nc.scalar.activation(out=lost[:], in_=minus_lost[:], func=COPY, scale=-1.0)
            nc.vector.tensor_tensor(h[b, t][:, g * BANK : (g + 1) * BANK], lost[:], idle[:], ALU.max)

        def less_done(b, t, g):
            part = h[b, t][:, g * BANK : (g + 1) * BANK]
            done = product((3,), b, t, g)
            nc.vector.tensor_tensor(part, part, done[:], ALU.subtract)

        def four_pass(b, t, g):
            idle_over_lost = product((1, 2), b, t, g)
            done_over_lost = product((1, 3), b, t, g)
            excess = staged(b, t, g)
            nc.scalar.activation(out=excess[:], in_=idle_over_lost[:], func=RELU)
            nc.vector.tensor_tensor(h[b, t][:, g * BANK : (g + 1) * BANK], excess[:], done_over_lost[:], ALU.subtract)

        x, planes, z_in, z_w, z_s = {}, {}, {}, {}, {}

        def pick(b, t, lo, n, after=None):
            x[b, t, lo] = held([P, n], F32, "x%d%d_%d" % (b, t, lo), after)
            window = h[b, t][:].indirect(offs2_sb[:, lo // PER_COLUMN : (lo + n) // PER_COLUMN])
            nc.vector.tensor_tensor(x[b, t, lo][:], window, wgt_sb[:, lo : lo + n], ALU.mult)
            if (b, lo) not in planes:
                planes[b, lo] = held([P, PACK, n], BF16, "planes%d_%d" % (b, lo))
            nc.scalar.activation(
                out=planes[b, lo][:, t, :], in_=x[b, t, lo][:], func=COPY, scale=gain_sb[:, b, t : t + 1]
            )

        def weave(b, lo, n):
            z_in[b, lo] = held([P, PACK * n], BF16, "z_in%d_%d" % (b, lo))
            nc.scalar.copy(
                out=z_in[b, lo][:].rearrange("p (c i t) -> p c t i", i=4, t=PACK),
                in_=planes[b, lo][:].rearrange("p t (c i) -> p c t i", i=4),
            )

        def quantize_z(b, lo, n):
            if b not in z_w:
                z_w[b] = held([P, M], U32, "z_w%d" % b)
                z_s[b] = held([P, M], U8, "z_s%d" % b)
            nc.vector.quantize_mx(
                out=z_w[b][:, lo : lo + n].bitcast(FP8X4), scales=z_s[b][:, lo : lo + n], in_=z_in[b, lo][:]
            )

        for g in range(HALVES):
            for t in range(PACK):
                if (t, g) == (LAST - 1, HALVES - 1):
                    quantize_weight(3, 0)
                larger(0, t, g)
        cast(1, 1)
        cast(3, 1)
        for t in range(PACK):
            less_done(0, t, 0)
            less_done(0, t, 1)
            if t > 0:
                pick(0, t - 1, 0, M)
            if t == 1:
                quantize_weight(1, 1)
            if t == 2:
                quantize_weight(3, 1)
        w4_w = held([P, RUNS * H], I32, "w4_w", after="raw_a")
        nc.sync.dma_start(
            out=w4_w[:].rearrange("p (a c) -> p a c", a=RUNS),
            in_=w4_words.rearrange("a p c j -> p a (c j)").bitcast(I32),
        )
        pick(0, LAST, 0, M)
        weave(0, 0, M)

        for t in range(PACK):
            if (1, t, 0) in FOUR_PASS:
                four_pass(1, t, 0)
                four_pass(1, t, 1)
            else:
                larger(1, t, 0)
                larger(1, t, 1)
                less_done(1, t, 0)
                less_done(1, t, 1)
            if t > 0:
                pick(1, t - 1, 0, HM)
        quantize_z(0, 0, M)
        pick(1, LAST, 0, HM)
        weave(1, 0, HM)

        w4_ds = held([P, H], U8, "w4_ds")
        deal(w4_ds[:], w_s[:])
        w4_dw = held([P, RUNS * H], I32, "w4_dw")
        nc.vector.tensor_copy(
            out=w4_dw[:].rearrange("p (ab t c i) -> p ab c t i", t=PACK, c=P // 4, i=4),
            in_=w4_w[:].rearrange("p (ab c i t) -> p ab c t i", t=PACK, c=P // 4, i=4),
        )
        quantize_z(1, 0, HM)
        freed_by_those_steps = ("w_s", "raw_a", "planes1_0", "z_in1_0")
        for t in range(PACK):
            pick(1, t, HM, HM, after=freed_by_those_steps[t])
        weave(1, HM, HM)

        rows = out.rearrange("(b p t) c -> b t p c", b=RUNS, t=PACK)

        def capped(b, t, lo, n, after=None):
            bank = psum.tile([P, BANK], F32, name="bank")
            c0 = b * RUN + t * P
            for a in range(RUNS):
                nc.tensor.matmul_mx(
                    out=bank[:, 0:n],
                    lhsT=w4_dw[:, a * H + c0 : a * H + c0 + P].bitcast(FP8X4),
                    lhsT_scale=w4_ds[4 + 4 * a : P, c0 : c0 + P],
                    rhs=z_w[a][:, lo : lo + n].bitcast(FP8X4),
                    rhs_scale=z_s[a][:, lo : lo + n],
                    start=(a == 0),
                    stop=(a == RUNS - 1),
                )
            if after:
                y = held([P, n], F32, "y_held", after)
            else:
                y = ring.tile([P, n], F32, name="y", bufs=Y_DEPTH, align_bytes=64)
            width = M if b == 0 else HM
            for c in range(0, n, width):
                nc.vector.tensor_tensor(y[:, c : c + width], x[b, t, lo + c][:], bank[:, c : c + width], ALU.min)
            return y

        def place(b, t, lo, n, y):
            window = pages[b, t][:].indirect(offs3_sb[:, lo // PER_COLUMN : (lo + n) // PER_COLUMN])
            nc.vector.tensor_tensor(window, y[:], wgo_sb[:, lo : lo + n], ALU.mult)
            if lo + n == M:
                nc.sync.dma_start(out=rows[b, t], in_=pages[b, t][:])

        halved = range(LAST)
        steps = [(1, t, lo, HM) for lo in (0, HM) for t in halved] + [(1, LAST, 0, M)]
        steps = steps + [(0, t, 0, M) for t in range(PACK)]
        pending = None
        for step in steps:
            if step == (1, halved[-1], 0, HM):
                quantize_z(1, HM, HM)
                y = capped(*step, after="z_in1_%d" % HM)
            else:
                y = capped(*step)
            if pending is not None:
                place(*pending)
            pending = step + (y,)
        place(*pending)
